import numpy as np
import ml_dtypes


def mxq(x, axis, fmt="e4m3"):
    dtype, down = {"e4m3": (ml_dtypes.float8_e4m3fn, 7), "e5m2": (ml_dtypes.float8_e5m2, 14)}[fmt]
    v = np.moveaxis(np.asarray(x, np.float32).astype(ml_dtypes.bfloat16).astype(np.float64), axis, -1)
    blocks = v.reshape(v.shape[:-1] + (-1, 32))
    amax = np.abs(blocks).max(-1, keepdims=True)
    byte = np.maximum(np.where(amax > 0, np.frexp(amax)[1] - 1 + 127, 0) - down, 1)
    scale = np.exp2(byte - 127.0)
    codes = (blocks / scale).astype(np.float32).astype(dtype).astype(np.float64)
    return np.moveaxis((codes * scale).reshape(v.shape), -1, axis)


WIDE = False


def mx_kscale(k):
    if not WIDE:
        return np.ones(k)
    levels = np.array([10, -10, 5, -5, 0])
    if k % 512:
        return np.exp2(np.random.permutation(np.resize(levels, k // 32))).repeat(32)
    a = np.empty((k // 512, 16))
    for p in range(k // 512):
        a[p, :8] = np.random.permutation(np.resize(levels, 8))
        for g in range(8):
            far = levels[np.abs(levels - a[p, g]) >= 10]
            a[p, g + 8] = far[np.random.randint(len(far))]
    return np.exp2(a.ravel()).repeat(32)


BF16 = ml_dtypes.bfloat16


def bf(x):
    return np.asarray(x, np.float32).astype(BF16)


def f64(x):
    return np.asarray(x).astype(np.float64)


T, N, W = 1024, 2048, 512


def l2_normalize_rows(x, gain):
    length = np.sqrt(np.sum(x * x, axis=-1, keepdims=True) + 1e-6)
    return gain * x / length


def softmax_last(x):
    shifted = x - np.max(x, axis=-1, keepdims=True)
    e = np.exp(shifted)
    return e / np.sum(e, axis=-1, keepdims=True)


def draw0():
    u, t = mx_kscale(W), mx_kscale(T)
    return {
        "key": bf(np.random.standard_normal((T, W)) / u),
        "mem": bf(np.random.standard_normal((N, W))),
        "gm": bf((1.0 + 0.1 * np.random.standard_normal(W)) * u),
        "s": bf(np.random.standard_normal(T) * t),
        "erase": bf((0.5 + 0.5 * np.random.standard_normal((T, W))) / t[:, None]),
        "add": bf(0.7 * np.random.standard_normal((T, W)) / t[:, None]),
    }


def core(key, mem, gm, s, erase, add):
    key, mem, gm, s, erase, add = f64(key), f64(mem), f64(gm), f64(s), f64(erase), f64(add)
    n_tokens = key.shape[0]
    n_rows = mem.shape[0]
    mn = l2_normalize_rows(mem, gm)
    cl = mxq(key, 1, "e4m3") @ mxq(mn, 1, "e4m3").T
    p = softmax_last(cl)
    scale = n_rows / np.sqrt(n_tokens)
    w = (s * scale)[:, None] * p
    wq = mxq(w, 0, "e4m3").T
    er = wq @ mxq(erase, 0, "e4m3")
    ad = wq @ mxq(add, 0, "e4m3")
    return mem * (1.0 - er) + ad


def e4m3fn_bytes(y):
    return np.clip(np.asarray(y, np.float64), -448.0, 448.0).astype(np.float32).astype(ml_dtypes.float8_e4m3fn).view(np.uint8)


def e4m3fn_values(b):
    return np.asarray(b, np.uint8).view(ml_dtypes.float8_e4m3fn).astype(np.float64)


def setup_inputs():
    d = draw0()
    x0 = np.asarray(d['key']).astype(np.float64)
    s = (np.max(np.abs(x0), axis=(0,), keepdims=True) / 448.0).astype(np.float32)
    out = {}
    for k, v in d.items():
        if k == 'key':
            out['key_bytes'] = e4m3fn_bytes(x0 / s.astype(np.float64))
            out['key_scale'] = s
        else:
            out[k] = v
    return out


def reference(key_bytes, key_scale, mem, gm, s, erase, add):
    return core(e4m3fn_values(key_bytes) * key_scale.astype(np.float64), mem, gm, s, erase, add)

@@ -1,0 +1,350 @@
+from contextlib import ExitStack
+
+import concourse.mybir as mybir
+from concourse.masks import make_identity
+
+T, N, W = 1024, 2048, 512
+FLOPS = 3 * 2 * T * N * W
+
+F32 = mybir.dt.float32
+BF16 = mybir.dt.bfloat16
+U32 = mybir.dt.uint32
+U8 = mybir.dt.uint8
+FP8 = mybir.dt.float8_e4m3fn
+FP8X4 = mybir.dt.float8_e4m3fn_x4
+ALU = mybir.AluOpType
+ACT = mybir.ActivationFunctionType
+X = mybir.AxisListType.X
+
+P = 128
+G = 2
+J = 4
+C = 4
+NTILES = 16
+
+OP2_GPSIMD = (0, 2, 4, 6, 8, 10, 12)
+COPY_V = ()
+
+
+def tile_ntmcontentaddresseraseadd_kernel(tc, key_bytes, key_scale, mem, gm, s, erase, add, out):
+    nc = tc.nc
+    with ExitStack() as ctx:
+        keep = ctx.enter_context(tc.tile_pool(name="keep", bufs=1))
+        ring = ctx.enter_context(tc.tile_pool(name="ring", bufs=2))
+        psum = ctx.enter_context(tc.psum_pool(name="psum", bufs=1))
+
+        ident_f = keep.tile([P, P], F32, name="ident_f")
+        ident_b = keep.tile([P, P], BF16, name="ident_b")
+        neg_half = keep.tile([P, C], F32, name="neg_half")
+        warm = keep.tile([P, 1], F32, name="warm")
+        warm_out = keep.tile([P, 1], F32, name="warm_out")
+        kscale = keep.tile([P, W], F32, name="kscale")
+        gain = keep.tile([P, W], BF16, name="gain")
+        s_raw = keep.tile([P, G, J], BF16, name="s_raw")
+        s64 = keep.tile([P, G * J], F32, name="s64")
+        kbytes = [keep.tile([P, J, W], U8, name=f"kbytes{g}") for g in range(G)]
+        memt = [keep.tile([P, C, W], BF16, name=f"mem{c}") for c in range(C)]
+        ea_raw = [keep.tile([P, J, W], BF16, name=f"ea_raw{i}") for i in range(4)]
+        junk = keep.tile([P, W], F32, name="junk")
+
+        kcodes = [keep.tile([P, 512], U32, name=f"kcodes{g}", align_bytes=64) for g in range(G)]
+        kplane = [keep.tile([P, 512], U8, name=f"kplane{g}", align_bytes=64) for g in range(G)]
+        mcodes = [keep.tile([P, 512], U32, name=f"mcodes{c}", align_bytes=64) for c in range(C)]
+        mplane = [keep.tile([P, 512], U8, name=f"mplane{c}", align_bytes=64) for c in range(C)]
+        eacodes = [keep.tile([P, W], U32, name=f"eacodes{i}", align_bytes=64) for i in range(4)]
+        eaplane = [keep.tile([P, W], U8, name=f"eaplane{i}", align_bytes=64) for i in range(4)]
+        wcodes = [[keep.tile([P, 512], U32, name=f"wcodes{g}_{c}", align_bytes=64) for c in range(C)] for g in range(G)]
+        wplane = [[keep.tile([P, 512], U8, name=f"wplane{g}_{c}", align_bytes=64) for c in range(C)] for g in range(G)]
+        w_bf = [[keep.tile([P, J, 512], BF16, name=f"w_bf{g}_{c}") for c in range(C)] for g in range(G)]
+
+        sumsq = [keep.tile([P, C], F32, name=f"sumsq{c}") for c in range(C)]
+        rnorm = [keep.tile([P, C], F32, name=f"rnorm{c}") for c in range(C)]
+        negmax4 = [keep.tile([P, C], F32, name=f"negmax4_{t}") for t in range(8)]
+        negmax = [keep.tile([P, 1], F32, name=f"negmax_{t}") for t in range(8)]
+        esum4 = [keep.tile([P, C], F32, name=f"esum4_{t}") for t in range(8)]
+        esum = [keep.tile([P, 1], F32, name=f"esum_{t}") for t in range(8)]
+        rsum = [keep.tile([P, 1], F32, name=f"rsum_{t}") for t in range(8)]
+
+        nc.gpsimd.memset(warm[:], 0.0)
+        make_identity(nc, ident_f[:])
+        nc.gpsimd.memset(neg_half[:], -0.5)
+        nc.gpsimd.tensor_copy(out=ident_b[:], in_=ident_f[:])
+
+        ctx.enter_context(tc.manual_schedule())
+
+        mem_v = mem.rearrange("(c p i) w -> c p i w", p=P, i=4)
+        out_v = out.rearrange("(c p i) w -> c p i w", p=P, i=4)
+        key_v = key_bytes.rearrange("(g p j) w -> g p j w", p=P, j=J)
+        er_v = erase.rearrange("(g p j) w -> g p j w", p=P, j=J)
+        ad_v = add.rearrange("(g p j) w -> g p j w", p=P, j=J)
+        ea_src = [er_v[0], ad_v[0], er_v[1], ad_v[1]]
+
+        nc.scalar.dma_start(out=gain[:], in_=gm.partition_broadcast(P))
+        nc.scalar.dma_start(out=kscale[:], in_=key_scale.rearrange("o k -> (o k)").partition_broadcast(P))
+        nc.sync.dma_start(out=memt[0][:, 0:2, :], in_=mem_v[0][:, 0:2, :])
+        nc.sync.dma_start(out=kbytes[0][:], in_=key_v[0])
+        nc.sync.dma_start(out=memt[0][:, 2:4, :], in_=mem_v[0][:, 2:4, :])
+        nc.sync.dma_start(out=memt[1][:], in_=mem_v[1])
+        nc.sync.dma_start(out=ea_raw[0][:], in_=ea_src[0])
+        nc.sync.dma_start(out=memt[2][:], in_=mem_v[2])
+        nc.sync.dma_start(out=ea_raw[1][:], in_=ea_src[1])
+        nc.sync.dma_start(out=memt[3][:], in_=mem_v[3])
+        nc.sync.dma_start(out=kbytes[1][:], in_=key_v[1])
+        nc.sync.dma_start(out=s_raw[:], in_=s.rearrange("(g p j) -> p g j", p=P, j=J))
+        nc.sync.dma_start(out=ea_raw[2][:], in_=ea_src[2])
+        nc.sync.dma_start(out=ea_raw[3][:], in_=ea_src[3])
+        nc.scalar.activation(out=warm_out[:], in_=warm[:], func=ACT.Exp)
+
+        def sum_squares(c):
+            for i in range(4):
+                nc.scalar.activation(out=junk[:], in_=memt[c][:, i, :], func=ACT.Square, accum_out=sumsq[c][:, i : i + 1])
+            nc.gpsimd.tensor_scalar(out=sumsq[c][:], in0=sumsq[c][:], scalar1=1e-6, scalar2=1.0, op0=ALU.add, op1=ALU.mult)
+            nc.gpsimd.tensor_tensor(out=rnorm[c][:], in0=sumsq[c][:], in1=neg_half[:], op=ALU.pow)
+
+        def transpose_in(rows):
+            words = rows[:].rearrange("p i k -> p (i k)").bitcast(F32)
+            banks = []
+            for b in range(2):
+                bank = psum.tile([P, 2, 2, P], F32, name="bank", tag="bank", bufs=8)
+                for a in range(2):
+                    for u in range(2):
+                        i = 2 * b + a
+                        nc.tensor.transpose(bank[:, a, u, :], words[:, 256 * i + u : 256 * (i + 1) : 2], ident_f[:])
+                banks.append(bank)
+            return banks
+
+        def copy_grouped(banks, grouped, which):
+            copy = nc.vector.tensor_copy if which in COPY_V else nc.scalar.copy
+            gw = grouped[:].rearrange("p n j -> p (n j)").bitcast(F32)
+            for b in range(2):
+                copy(
+                    out=gw[:, 512 * b : 512 * (b + 1)].rearrange("p (a r u) -> p a r u", a=2, u=2),
+                    in_=banks[b][:].rearrange("p a u r -> p a r u"),
+                )
+
+        def quantize(grouped, codes, plane):
+            nc.vector.quantize_mx(out=codes[:].bitcast(FP8X4), scales=plane[:], in_=grouped[:].rearrange("p n j -> p (n j)"))
+
+        def key_widen(g):
+            rows = ring.tile([P, J, W], BF16, name="key_rows", tag="rows", bufs=2)
+            for j in range(J):
+                nc.vector.tensor_tensor(out=rows[:, j, :], in0=kbytes[g][:, j, :].bitcast(FP8), in1=kscale[:], op=ALU.mult)
+            return rows
+
+        def mem_norm(c):
+            rows = ring.tile([P, J, W], BF16, name="mem_rows", tag="rows", bufs=2)
+            for i in range(4):
+                nc.vector.scalar_tensor_tensor(
+                    out=rows[:, i, :], in0=memt[c][:, i, :], scalar=rnorm[c][:, i : i + 1], in1=gain[:], op0=ALU.mult, op1=ALU.mult
+                )
+            return rows
+
+        def new_grouped():
+            g4 = ring.tile([P, 512, 4], BF16, name="grouped", tag="grouped", bufs=3, align_bytes=64)
+            return g4
+
+        cl = {}
+
+        def logits(t):
+            g, j = divmod(t, J)
+            for c in range(C):
+                bank = psum.tile([P, 512], F32, name="bank", tag="bank", bufs=8)
+                nc.tensor.matmul_mx(
+                    out=bank[:],
+                    lhsT=kcodes[g][:, 128 * j : 128 * (j + 1)].bitcast(FP8X4),
+                    lhsT_scale=kplane[g][:, 128 * j : 128 * (j + 1)],
+                    rhs=mcodes[c][:].bitcast(FP8X4),
+                    rhs_scale=mplane[c][:],
+                    start=True,
+                    stop=True,
+                )
+                cl[t, c] = bank
+
+        def row_max(t):
+            for c in range(C):
+                nc.vector.tensor_reduce(out=negmax4[t][:, c : c + 1], in_=cl[t, c][:], axis=X, op=ALU.max, negate=True)
+            nc.vector.tensor_reduce(out=negmax[t][:], in_=negmax4[t][:], axis=X, op=ALU.min)
+
+        exps = {}
+
+        def exponentials(t):
+            e = ring.tile([P, C, 512], F32, name="e", tag="e", bufs=3)
+            exps[t] = e
+            for c in range(C):
+                nc.scalar.activation(
+                    out=e[:, c, :], in_=cl[t, c][:], func=ACT.Exp, bias=negmax[t][:], scale=1.0, accum_out=esum4[t][:, c : c + 1]
+                )
+
+        def row_sum(t):
+            nc.vector.tensor_reduce(out=esum[t][:], in_=esum4[t][:], axis=X, op=ALU.add)
+            nc.vector.reciprocal(out=rsum[t][:], in_=esum[t][:])
+
+        def weights(t, engine, chunks):
+            g, j = divmod(t, J)
+            for c in chunks:
+                engine.tensor_scalar(
+                    out=w_bf[g][c][:, j, :], in0=exps[t][:, c, :], scalar1=rsum[t][:], scalar2=s64[:, t : t + 1], op0=ALU.mult, op1=ALU.mult
+                )
+
+        def pe_interleave(rows, copies=(nc.scalar.copy, nc.scalar.copy)):
+            g4 = new_grouped()
+            for h in range(2):
+                bank = psum.tile([P, 2, P, J], BF16, name="ilbank", tag="bank", bufs=8)
+                for q in range(2):
+                    col = 256 * h + 128 * q
+                    nc.tensor.matmul(
+                        out=bank[:, q, :, :],
+                        lhsT=ident_b[:],
+                        rhs=rows[:, :, col : col + 128].rearrange("p j n -> p n j"),
+                        start=True,
+                        stop=True,
+                    )
+                copies[h](
+                    out=g4[:, 256 * h : 256 * (h + 1), :].rearrange("p n j -> p (n j)"), in_=bank[:].rearrange("p q n j -> p (q n j)")
+                )
+            return g4
+
+        def w_interleave(copy, g, c, g4, h):
+            copy(out=g4[:, 256 * h : 256 * (h + 1), :], in_=w_bf[g][c][:, :, 256 * h : 256 * (h + 1)].rearrange("p j n -> p n j"))
+
+        def quantize_half(g4, codes, plane, h):
+            nc.vector.quantize_mx(
+                out=codes[:, 256 * h : 256 * (h + 1)].bitcast(FP8X4),
+                scales=plane[:, 256 * h : 256 * (h + 1)],
+                in_=g4[:, 256 * h : 256 * (h + 1), :].rearrange("p n j -> p (n j)"),
+            )
+
+        SS, VV = nc.scalar.copy, nc.vector.tensor_copy
+        sum_squares(0)
+        krows = key_widen(0)
+        sum_squares(1)
+        kb = transpose_in(krows)
+        kgrp = new_grouped()
+        copy_grouped(kb, kgrp, "k0")
+        mrows = mem_norm(0)
+        mb = transpose_in(mrows)
+        quantize(kgrp, kcodes[0], kplane[0])
+        nc.gpsimd.tensor_scalar(
+            out=s64[:], in0=s_raw[:].rearrange("p g j -> p (g j)"), scalar1=64.0, scalar2=0.0, op0=ALU.mult, op1=ALU.add
+        )
+        for c in range(1, C):
+            if c + 1 < C:
+                sum_squares(c + 1)
+            mrows = mem_norm(c)
+            mgrp = new_grouped()
+            copy_grouped(mb, mgrp, f"m{c - 1}")
+            eag = pe_interleave(ea_raw[c - 1])
+            mb = transpose_in(mrows)
+            quantize(mgrp, mcodes[c - 1], mplane[c - 1])
+            quantize(eag, eacodes[c - 1], eaplane[c - 1])
+        mgrp = new_grouped()
+        copy_grouped(mb, mgrp, "m3")
+        krows = key_widen(1)
+        quantize(mgrp, mcodes[3], mplane[3])
+        logits(0)
+        kb = transpose_in(krows)
+        kgrp = new_grouped()
+        copy_grouped(kb, kgrp, "k1")
+
+        grp = {}
+        for t in range(8):
+            row_max(t)
+            if t == 0:
+                quantize(kgrp, kcodes[1], kplane[1])
+            if t + 1 < 8:
+                logits(t + 1)
+            exponentials(t)
+            if t > 0:
+                row_sum(t - 1)
+                weights(t - 1, nc.gpsimd, range(C))
+            if t == 0:
+                eag = pe_interleave(ea_raw[3])
+            if t == 1:
+                quantize(eag, eacodes[3], eaplane[3])
+            if t == 5:
+                grp[0, 0] = pe_interleave(w_bf[0][0], (SS, SS))
+            if t == 6:
+                quantize(grp[0, 0], wcodes[0][0], wplane[0][0])
+                grp[0, 1] = pe_interleave(w_bf[0][1], (SS, SS))
+            if t == 7:
+                quantize(grp[0, 1], wcodes[0][1], wplane[0][1])
+                grp[0, 2] = pe_interleave(w_bf[0][2], (SS, VV))
+                quantize(grp[0, 2], wcodes[0][2], wplane[0][2])
+        grp[0, 3] = pe_interleave(w_bf[0][3], (SS, SS))
+        row_sum(7)
+        weights(7, nc.vector, range(0, 2))
+        grp[1, 0] = new_grouped()
+        w_interleave(VV, 1, 0, grp[1, 0], 0)
+        grp[1, 1] = new_grouped()
+        w_interleave(SS, 1, 1, grp[1, 1], 0)
+        w_interleave(SS, 1, 1, grp[1, 1], 1)
+        quantize_half(grp[1, 0], wcodes[1][0], wplane[1][0], 0)
+        weights(7, nc.vector, range(2, 4))
+        w_interleave(VV, 1, 0, grp[1, 0], 1)
+        quantize_half(grp[1, 0], wcodes[1][0], wplane[1][0], 1)
+        quantize(grp[0, 3], wcodes[0][3], wplane[0][3])
+
+        acc = {}
+
+        def open_tile(m):
+            for k in range(2):
+                acc[m, k] = psum.tile([P, 512], F32, name="acc", tag="bank", bufs=8)
+
+        def write_pass(m, g):
+            c, i = divmod(m, 4)
+            for k in range(2):
+                nc.tensor.matmul_mx(
+                    out=acc[m, k][:],
+                    lhsT=wcodes[g][c][:, 128 * i : 128 * (i + 1)].bitcast(FP8X4),
+                    lhsT_scale=wplane[g][c][:, 128 * i : 128 * (i + 1)],
+                    rhs=eacodes[2 * g + k][:].bitcast(FP8X4),
+                    rhs_scale=eaplane[2 * g + k][:],
+                    start=(g == 0),
+                    stop=(g == 1),
+                )
+
+        erased = {}
+        results = {}
+
+        def finish_a(m):
+            c, i = divmod(m, 4)
+            if i % 2 == 0:
+                results[m // 2] = ring.tile([P, 2, 512], F32, name="result", tag="result", bufs=3)
+            erased[m] = ring.tile([P, 512], F32, name="erased", tag="erased", bufs=4)
+            nc.vector.scalar_tensor_tensor(
+                out=erased[m][:], in0=acc[m, 0][:], scalar=1.0, in1=memt[c][:, i, :], op0=ALU.subtract, op1=ALU.mult
+            )
+            if m in OP2_GPSIMD:
+                added = ring.tile([P, 512], F32, name="added", tag="added", bufs=3)
+                nc.scalar.copy(out=added[:], in_=acc[m, 1][:])
+                acc[m, 1] = added
+
+        def finish_b(m):
+            c, i = divmod(m, 4)
+            engine = nc.gpsimd if m in OP2_GPSIMD else nc.vector
+            engine.tensor_tensor(out=results[m // 2][:, i % 2, :], in0=acc[m, 1][:], in1=erased[m][:], op=ALU.subtract)
+            if m >= 14:
+                nc.sync.dma_start(out=out_v[c][:, i, :], in_=results[m // 2][:, i % 2, :])
+            elif i % 2 == 1:
+                nc.sync.dma_start(out=out_v[c][:, i - 1 : i + 1, :], in_=results[m // 2][:])
+
+        for m in range(4):
+            open_tile(m)
+            write_pass(m, 0)
+        for m in range(NTILES):
+            c, i = divmod(m, 4)
+            if m >= 4:
+                open_tile(m)
+                write_pass(m, 0)
+            write_pass(m, 1)
+            finish_a(m)
+            if m > 0:
+                finish_b(m - 1)
+            if m in (0, 1, 4, 5):
+                nxt = 2 if m < 4 else 3
+                if m in (0, 4):
+                    grp[1, nxt] = new_grouped()
+                w_interleave(SS, 1, nxt, grp[1, nxt], m % 4)
+            if i == 2 and c + 1 < C:
+                quantize(grp[1, c + 1], wcodes[1][c + 1], wplane[1][c + 1])
+        finish_b(15)

@@ -35,11 +35,13 @@ def tile_ntmcontentaddresseraseadd_kernel(tc, key_bytes, key_scale, mem, gm, s, 
 
         ident_f = keep.tile([P, P], F32, name="ident_f")
         ident_b = keep.tile([P, P], BF16, name="ident_b")
-        neg_half = keep.tile([P, C], F32, name="neg_half")
+        eps = keep.tile([P, 1], F32, name="eps")
         warm = keep.tile([P, 1], F32, name="warm")
         warm_out = keep.tile([P, 1], F32, name="warm_out")
-        kscale = keep.tile([P, W], F32, name="kscale")
+        kscale = keep.tile([P, 2, 2], F32, name="kscale")
         gain = keep.tile([P, W], BF16, name="gain")
+        gain_row = keep.tile([P, W], BF16, name="gain_row")
+        ones = keep.tile([P, P], BF16, name="ones")
         s_raw = keep.tile([P, G, J], BF16, name="s_raw")
         s64 = keep.tile([P, G * J], F32, name="s64")
         kbytes = [keep.tile([P, J, W], U8, name=f"kbytes{g}") for g in range(G)]
@@ -58,6 +60,7 @@ def tile_ntmcontentaddresseraseadd_kernel(tc, key_bytes, key_scale, mem, gm, s, 
         w_bf = [[keep.tile([P, J, 512], BF16, name=f"w_bf{g}_{c}") for c in range(C)] for g in range(G)]
 
         sumsq = [keep.tile([P, C], F32, name=f"sumsq{c}") for c in range(C)]
+        length = [keep.tile([P, C], F32, name=f"length{c}") for c in range(C)]
         rnorm = [keep.tile([P, C], F32, name=f"rnorm{c}") for c in range(C)]
         negmax4 = [keep.tile([P, C], F32, name=f"negmax4_{t}") for t in range(8)]
         negmax = [keep.tile([P, 1], F32, name=f"negmax_{t}") for t in range(8)]
@@ -65,9 +68,9 @@ def tile_ntmcontentaddresseraseadd_kernel(tc, key_bytes, key_scale, mem, gm, s, 
         esum = [keep.tile([P, 1], F32, name=f"esum_{t}") for t in range(8)]
         rsum = [keep.tile([P, 1], F32, name=f"rsum_{t}") for t in range(8)]
 
-        nc.gpsimd.memset(warm[:], 0.0)
+        nc.vector.memset(warm[:], 0.0)
+        nc.vector.memset(eps[:], 1e-6)
         make_identity(nc, ident_f[:])
-        nc.gpsimd.memset(neg_half[:], -0.5)
         nc.gpsimd.tensor_copy(out=ident_b[:], in_=ident_f[:])
 
         ctx.enter_context(tc.manual_schedule())
@@ -79,8 +82,11 @@ def tile_ntmcontentaddresseraseadd_kernel(tc, key_bytes, key_scale, mem, gm, s, 
         ad_v = add.rearrange("(g p j) w -> g p j w", p=P, j=J)
         ea_src = [er_v[0], ad_v[0], er_v[1], ad_v[1]]
 
-        nc.scalar.dma_start(out=gain[:], in_=gm.partition_broadcast(P))
-        nc.scalar.dma_start(out=kscale[:], in_=key_scale.rearrange("o k -> (o k)").partition_broadcast(P))
+        nc.vector.memset(gain_row[:], 0.0)
+        nc.vector.memset(ones[:], 1.0)
+        nc.scalar.dma_start(out=kscale[:], in_=key_scale.rearrange("o (p u e) -> p (o u) e", p=P, u=2))
+        nc.scalar.dma_start(out=gain_row[0:1, :], in_=gm.rearrange("(o k) -> o k", o=1))
+        nc.scalar.dma_start(out=s_raw[:], in_=s.rearrange("(g p j) -> p g j", p=P, j=J))
         nc.sync.dma_start(out=memt[0][:, 0:2, :], in_=mem_v[0][:, 0:2, :])
         nc.sync.dma_start(out=kbytes[0][:], in_=key_v[0])
         nc.sync.dma_start(out=memt[0][:, 2:4, :], in_=mem_v[0][:, 2:4, :])
@@ -90,16 +96,19 @@ def tile_ntmcontentaddresseraseadd_kernel(tc, key_bytes, key_scale, mem, gm, s, 
         nc.sync.dma_start(out=ea_raw[1][:], in_=ea_src[1])
         nc.sync.dma_start(out=memt[3][:], in_=mem_v[3])
         nc.sync.dma_start(out=kbytes[1][:], in_=key_v[1])
-        nc.sync.dma_start(out=s_raw[:], in_=s.rearrange("(g p j) -> p g j", p=P, j=J))
         nc.sync.dma_start(out=ea_raw[2][:], in_=ea_src[2])
         nc.sync.dma_start(out=ea_raw[3][:], in_=ea_src[3])
-        nc.scalar.activation(out=warm_out[:], in_=warm[:], func=ACT.Exp)
+        nc.scalar.activation(out=warm_out[:], in_=warm[:], func=ACT.Sqrt)
 
         def sum_squares(c):
             for i in range(4):
                 nc.scalar.activation(out=junk[:], in_=memt[c][:, i, :], func=ACT.Square, accum_out=sumsq[c][:, i : i + 1])
-            nc.gpsimd.tensor_scalar(out=sumsq[c][:], in0=sumsq[c][:], scalar1=1e-6, scalar2=1.0, op0=ALU.add, op1=ALU.mult)
-            nc.gpsimd.tensor_tensor(out=rnorm[c][:], in0=sumsq[c][:], in1=neg_half[:], op=ALU.pow)
+
+        def rnorms_s(c):
+            nc.scalar.activation(out=length[c][:], in_=sumsq[c][:], func=ACT.Sqrt, bias=eps[:], scale=1.0)
+
+        def rnorms_v(c):
+            nc.vector.reciprocal(out=rnorm[c][:], in_=length[c][:])
 
         def transpose_in(rows):
             words = rows[:].rearrange("p i k -> p (i k)").bitcast(F32)
@@ -126,13 +135,24 @@ def tile_ntmcontentaddresseraseadd_kernel(tc, key_bytes, key_scale, mem, gm, s, 
             nc.vector.quantize_mx(out=codes[:].bitcast(FP8X4), scales=plane[:], in_=grouped[:].rearrange("p n j -> p (n j)"))
 
         def key_widen(g):
-            rows = ring.tile([P, J, W], BF16, name="key_rows", tag="rows", bufs=2)
-            for j in range(J):
-                nc.vector.tensor_tensor(out=rows[:, j, :], in0=kbytes[g][:, j, :].bitcast(FP8), in1=kscale[:], op=ALU.mult)
+            rows = ring.tile([P, J, W], BF16, name="key_rows", tag="rows", bufs=3)
+            cast = nc.vector.tensor_copy if g == 0 else nc.scalar.copy
+            cast(out=rows[:].rearrange("p j w -> p (j w)"), in_=kbytes[g][:].rearrange("p j w -> p (j w)").bitcast(FP8))
             return rows
 
+        def key_scale_out(banks, g4):
+            for b in range(2):
+                for a in range(2):
+                    n0 = 128 * (2 * b + a)
+                    nc.vector.tensor_tensor(
+                        out=g4[:, n0 : n0 + 128, :].rearrange("p r (u e) -> p r u e", u=2),
+                        in0=banks[b][:, a, :, :].bitcast(BF16).rearrange("p u (r e) -> p r u e", e=2),
+                        in1=kscale[:].unsqueeze(1).to_broadcast([P, P, 2, 2]),
+                        op=ALU.mult,
+                    )
+
         def mem_norm(c):
-            rows = ring.tile([P, J, W], BF16, name="mem_rows", tag="rows", bufs=2)
+            rows = ring.tile([P, J, W], BF16, name="mem_rows", tag="rows", bufs=3)
             for i in range(4):
                 nc.vector.scalar_tensor_tensor(
                     out=rows[:, i, :], in0=memt[c][:, i, :], scalar=rnorm[c][:, i : i + 1], in1=gain[:], op0=ALU.mult, op1=ALU.mult
@@ -140,14 +160,14 @@ def tile_ntmcontentaddresseraseadd_kernel(tc, key_bytes, key_scale, mem, gm, s, 
             return rows
 
         def new_grouped():
-            g4 = ring.tile([P, 512, 4], BF16, name="grouped", tag="grouped", bufs=3, align_bytes=64)
+            g4 = ring.tile([P, 512, 4], BF16, name="grouped", tag="grouped", bufs=6, align_bytes=64)
             return g4
 
         cl = {}
 
-        def logits(t):
+        def logits(t, chunks=range(C)):
             g, j = divmod(t, J)
-            for c in range(C):
+            for c in chunks:
                 bank = psum.tile([P, 512], F32, name="bank", tag="bank", bufs=8)
                 nc.tensor.matmul_mx(
                     out=bank[:],
@@ -160,9 +180,10 @@ def tile_ntmcontentaddresseraseadd_kernel(tc, key_bytes, key_scale, mem, gm, s, 
                 )
                 cl[t, c] = bank
 
+        def bank_max(t, c):
+            nc.vector.tensor_reduce(out=negmax4[t][:, c : c + 1], in_=cl[t, c][:], axis=X, op=ALU.max, negate=True)
+
         def row_max(t):
-            for c in range(C):
-                nc.vector.tensor_reduce(out=negmax4[t][:, c : c + 1], in_=cl[t, c][:], axis=X, op=ALU.max, negate=True)
             nc.vector.tensor_reduce(out=negmax[t][:], in_=negmax4[t][:], axis=X, op=ALU.min)
 
         exps = {}
@@ -177,6 +198,8 @@ def tile_ntmcontentaddresseraseadd_kernel(tc, key_bytes, key_scale, mem, gm, s, 
 
         def row_sum(t):
             nc.vector.tensor_reduce(out=esum[t][:], in_=esum4[t][:], axis=X, op=ALU.add)
+
+        def row_recip(t):
             nc.vector.reciprocal(out=rsum[t][:], in_=esum[t][:])
 
         def weights(t, engine, chunks):
@@ -186,8 +209,8 @@ def tile_ntmcontentaddresseraseadd_kernel(tc, key_bytes, key_scale, mem, gm, s, 
                     out=w_bf[g][c][:, j, :], in0=exps[t][:, c, :], scalar1=rsum[t][:], scalar2=s64[:, t : t + 1], op0=ALU.mult, op1=ALU.mult
                 )
 
-        def pe_interleave(rows, copies=(nc.scalar.copy, nc.scalar.copy)):
-            g4 = new_grouped()
+        def pe_interleave(rows):
+            banks = []
             for h in range(2):
                 bank = psum.tile([P, 2, P, J], BF16, name="ilbank", tag="bank", bufs=8)
                 for q in range(2):
@@ -199,10 +222,13 @@ def tile_ntmcontentaddresseraseadd_kernel(tc, key_bytes, key_scale, mem, gm, s, 
                         start=True,
                         stop=True,
                     )
-                copies[h](
-                    out=g4[:, 256 * h : 256 * (h + 1), :].rearrange("p n j -> p (n j)"), in_=bank[:].rearrange("p q n j -> p (q n j)")
-                )
-            return g4
+                banks.append(bank)
+            return banks
+
+        def copy_interleaved(banks, g4, h, copy):
+            copy(
+                out=g4[:, 256 * h : 256 * (h + 1), :].rearrange("p n j -> p (n j)"), in_=banks[h][:].rearrange("p q n j -> p (q n j)")
+            )
 
         def w_interleave(copy, g, c, g4, h):
             copy(out=g4[:, 256 * h : 256 * (h + 1), :], in_=w_bf[g][c][:, :, 256 * h : 256 * (h + 1)].rearrange("p j n -> p n j"))
@@ -215,63 +241,119 @@ def tile_ntmcontentaddresseraseadd_kernel(tc, key_bytes, key_scale, mem, gm, s, 
             )
 
         SS, VV = nc.scalar.copy, nc.vector.tensor_copy
+        kb, kgrp, mb, mgrp, eab, eag, wb, wg = {}, {}, {}, {}, {}, {}, {}, {}
+
+        def copy_out(kind, x):
+            if kind == "k":
+                kgrp[x] = new_grouped()
+                key_scale_out(kb[x], kgrp[x])
+            else:
+                mgrp[x] = new_grouped()
+                copy_grouped(mb[x], mgrp[x], f"{kind}{x}")
+
+        def ea_pe(i):
+            eab[i] = pe_interleave(ea_raw[i])
+
+        def ea_copy(i, engines=None):
+            engines = engines or (SS, SS)
+            eag[i] = new_grouped()
+            for h in range(2):
+                copy_interleaved(eab[i], eag[i], h, engines[h])
+
+        def ea_quant(i):
+            quantize(eag[i], eacodes[i], eaplane[i])
+
+        def w_pe(c):
+            wb[c] = pe_interleave(w_bf[0][c])
+
+        def w_copy(c, engines=None):
+            engines = engines or (SS, SS)
+            wg[c] = new_grouped()
+            for h in range(2):
+                copy_interleaved(wb[c], wg[c], h, engines[h])
+
+        def w_quant(c):
+            quantize(wg[c], wcodes[0][c], wplane[0][c])
+
+        gbank = psum.tile([P, W], F32, name="gbank", tag="bank", bufs=8)
+        nc.tensor.matmul(out=gbank[:], lhsT=ones[:], rhs=gain_row[:], start=True, stop=True)
+        krows0 = key_widen(0)
+        nc.vector.tensor_copy(out=gain[:], in_=gbank[:])
         sum_squares(0)
-        krows = key_widen(0)
+        rnorms_s(0)
         sum_squares(1)
-        kb = transpose_in(krows)
-        kgrp = new_grouped()
-        copy_grouped(kb, kgrp, "k0")
-        mrows = mem_norm(0)
-        mb = transpose_in(mrows)
-        quantize(kgrp, kcodes[0], kplane[0])
+        rnorms_s(1)
+        kb[0] = transpose_in(krows0)
+        copy_out("k", 0)
+        rnorms_v(0)
+        mb[0] = transpose_in(mem_norm(0))
+        quantize(kgrp[0], kcodes[0], kplane[0])
         nc.gpsimd.tensor_scalar(
             out=s64[:], in0=s_raw[:].rearrange("p g j -> p (g j)"), scalar1=64.0, scalar2=0.0, op0=ALU.mult, op1=ALU.add
         )
-        for c in range(1, C):
-            if c + 1 < C:
-                sum_squares(c + 1)
-            mrows = mem_norm(c)
-            mgrp = new_grouped()
-            copy_grouped(mb, mgrp, f"m{c - 1}")
-            eag = pe_interleave(ea_raw[c - 1])
-            mb = transpose_in(mrows)
-            quantize(mgrp, mcodes[c - 1], mplane[c - 1])
-            quantize(eag, eacodes[c - 1], eaplane[c - 1])
-        mgrp = new_grouped()
-        copy_grouped(mb, mgrp, "m3")
-        krows = key_widen(1)
-        quantize(mgrp, mcodes[3], mplane[3])
-        logits(0)
-        kb = transpose_in(krows)
-        kgrp = new_grouped()
-        copy_grouped(kb, kgrp, "k1")
-
-        grp = {}
+        sum_squares(2)
+        rnorms_s(2)
+        copy_out("m", 0)
+        rnorms_v(1)
+        mb[1] = transpose_in(mem_norm(1))
+        sum_squares(3)
+        rnorms_s(3)
+        rnorms_v(2)
+        mb[2] = transpose_in(mem_norm(2))
+        quantize(mgrp[0], mcodes[0], mplane[0])
+        copy_out("m", 1)
+        nc.scalar.activation(out=warm_out[:], in_=warm[:], func=ACT.Exp)
+        ea_pe(0)
+        krows1 = key_widen(1)
+        rnorms_v(3)
+        logits(0, [0])
+        mb[3] = transpose_in(mem_norm(3))
+        copy_out("m", 2)
+        quantize(mgrp[1], mcodes[1], mplane[1])
+        ea_copy(0)
+        copy_out("m", 3)
+        quantize(mgrp[2], mcodes[2], mplane[2])
+        logits(0, [1, 2])
+        kb[1] = transpose_in(krows1)
+        bank_max(0, 0)
+        bank_max(0, 1)
+        quantize(mgrp[3], mcodes[3], mplane[3])
+        bank_max(0, 2)
+        logits(0, [3])
+        ea_pe(1)
+        ea_copy(1)
         for t in range(8):
+            for c in range(C):
+                if (t, c) not in ((0, 0), (0, 1), (0, 2)):
+                    bank_max(t, c)
+            if t > 0:
+                row_sum(t - 1)
             row_max(t)
-            if t == 0:
-                quantize(kgrp, kcodes[1], kplane[1])
+            if t > 0:
+                row_recip(t - 1)
+                weights(t - 1, nc.gpsimd, range(C))
             if t + 1 < 8:
                 logits(t + 1)
             exponentials(t)
-            if t > 0:
-                row_sum(t - 1)
-                weights(t - 1, nc.gpsimd, range(C))
             if t == 0:
-                eag = pe_interleave(ea_raw[3])
+                copy_out("k", 1)
             if t == 1:
-                quantize(eag, eacodes[3], eaplane[3])
-            if t == 5:
-                grp[0, 0] = pe_interleave(w_bf[0][0], (SS, SS))
-            if t == 6:
-                quantize(grp[0, 0], wcodes[0][0], wplane[0][0])
-                grp[0, 1] = pe_interleave(w_bf[0][1], (SS, SS))
+                quantize(kgrp[1], kcodes[1], kplane[1])
+            if 1 <= t <= 2:
+                ea_pe(t + 1)
+                ea_copy(t + 1)
+            if 2 <= t <= 5:
+                ea_quant(t - 2)
+            if t >= 5:
+                w_pe(t - 5)
+                w_copy(t - 5)
             if t == 7:
-                quantize(grp[0, 1], wcodes[0][1], wplane[0][1])
-                grp[0, 2] = pe_interleave(w_bf[0][2], (SS, VV))
-                quantize(grp[0, 2], wcodes[0][2], wplane[0][2])
-        grp[0, 3] = pe_interleave(w_bf[0][3], (SS, SS))
+                w_quant(0)
+        w_pe(3)
+        w_copy(3)
         row_sum(7)
+        row_recip(7)
+        grp = {}
         weights(7, nc.vector, range(0, 2))
         grp[1, 0] = new_grouped()
         w_interleave(VV, 1, 0, grp[1, 0], 0)
@@ -282,7 +364,7 @@ def tile_ntmcontentaddresseraseadd_kernel(tc, key_bytes, key_scale, mem, gm, s, 
         weights(7, nc.vector, range(2, 4))
         w_interleave(VV, 1, 0, grp[1, 0], 1)
         quantize_half(grp[1, 0], wcodes[1][0], wplane[1][0], 1)
-        quantize(grp[0, 3], wcodes[0][3], wplane[0][3])
+        w_quant(1)
 
         acc = {}
 
@@ -337,14 +419,16 @@ def tile_ntmcontentaddresseraseadd_kernel(tc, key_bytes, key_scale, mem, gm, s, 
                 open_tile(m)
                 write_pass(m, 0)
             write_pass(m, 1)
+            if i == 1 and c + 1 < C:
+                quantize(grp[1, c + 1], wcodes[1][c + 1], wplane[1][c + 1])
             finish_a(m)
             if m > 0:
                 finish_b(m - 1)
-            if m in (0, 1, 4, 5):
-                nxt = 2 if m < 4 else 3
-                if m in (0, 4):
+            if m in (2, 5):
+                w_quant(2 if m == 2 else 3)
+            if m in (0, 1, 2, 3):
+                nxt = 2 if m < 2 else 3
+                if m in (0, 2):
                     grp[1, nxt] = new_grouped()
-                w_interleave(SS, 1, nxt, grp[1, nxt], m % 4)
-            if i == 2 and c + 1 < C:
-                quantize(grp[1, c + 1], wcodes[1][c + 1], wplane[1][c + 1])
+                w_interleave(SS, 1, nxt, grp[1, nxt], m % 2)
         finish_b(15)

from contextlib import ExitStack

import concourse.mybir as mybir
from concourse.masks import make_identity

T, N, W = 1024, 2048, 512
FLOPS = 3 * 2 * T * N * W

F32 = mybir.dt.float32
BF16 = mybir.dt.bfloat16
U32 = mybir.dt.uint32
U8 = mybir.dt.uint8
FP8 = mybir.dt.float8_e4m3fn
FP8X4 = mybir.dt.float8_e4m3fn_x4
ALU = mybir.AluOpType
ACT = mybir.ActivationFunctionType
X = mybir.AxisListType.X

P = 128
G = 2
J = 4
C = 4
NTILES = 16

OP2_GPSIMD = (0, 2, 4, 6, 8, 10, 12)
COPY_V = ()


def tile_ntmcontentaddresseraseadd_kernel(tc, key_bytes, key_scale, mem, gm, s, erase, add, out):
    nc = tc.nc
    with ExitStack() as ctx:
        keep = ctx.enter_context(tc.tile_pool(name="keep", bufs=1))
        ring = ctx.enter_context(tc.tile_pool(name="ring", bufs=2))
        psum = ctx.enter_context(tc.psum_pool(name="psum", bufs=1))

        ident_f = keep.tile([P, P], F32, name="ident_f")
        ident_b = keep.tile([P, P], BF16, name="ident_b")
        eps = keep.tile([P, 1], F32, name="eps")
        warm = keep.tile([P, 1], F32, name="warm")
        warm_out = keep.tile([P, 1], F32, name="warm_out")
        kscale = keep.tile([P, 2, 2], F32, name="kscale")
        gain = keep.tile([P, W], BF16, name="gain")
        gain_row = keep.tile([P, W], BF16, name="gain_row")
        ones = keep.tile([P, P], BF16, name="ones")
        s_raw = keep.tile([P, G, J], BF16, name="s_raw")
        s64 = keep.tile([P, G * J], F32, name="s64")
        kbytes = [keep.tile([P, J, W], U8, name=f"kbytes{g}") for g in range(G)]
        memt = [keep.tile([P, C, W], BF16, name=f"mem{c}") for c in range(C)]
        ea_raw = [keep.tile([P, J, W], BF16, name=f"ea_raw{i}") for i in range(4)]
        junk = keep.tile([P, W], F32, name="junk")

        kcodes = [keep.tile([P, 512], U32, name=f"kcodes{g}", align_bytes=64) for g in range(G)]
        kplane = [keep.tile([P, 512], U8, name=f"kplane{g}", align_bytes=64) for g in range(G)]
        mcodes = [keep.tile([P, 512], U32, name=f"mcodes{c}", align_bytes=64) for c in range(C)]
        mplane = [keep.tile([P, 512], U8, name=f"mplane{c}", align_bytes=64) for c in range(C)]
        eacodes = [keep.tile([P, W], U32, name=f"eacodes{i}", align_bytes=64) for i in range(4)]
        eaplane = [keep.tile([P, W], U8, name=f"eaplane{i}", align_bytes=64) for i in range(4)]
        wcodes = [[keep.tile([P, 512], U32, name=f"wcodes{g}_{c}", align_bytes=64) for c in range(C)] for g in range(G)]
        wplane = [[keep.tile([P, 512], U8, name=f"wplane{g}_{c}", align_bytes=64) for c in range(C)] for g in range(G)]
        w_bf = [[keep.tile([P, J, 512], BF16, name=f"w_bf{g}_{c}") for c in range(C)] for g in range(G)]

        sumsq = [keep.tile([P, C], F32, name=f"sumsq{c}") for c in range(C)]
        length = [keep.tile([P, C], F32, name=f"length{c}") for c in range(C)]
        rnorm = [keep.tile([P, C], F32, name=f"rnorm{c}") for c in range(C)]
        negmax4 = [keep.tile([P, C], F32, name=f"negmax4_{t}") for t in range(8)]
        negmax = [keep.tile([P, 1], F32, name=f"negmax_{t}") for t in range(8)]
        esum4 = [keep.tile([P, C], F32, name=f"esum4_{t}") for t in range(8)]
        esum = [keep.tile([P, 1], F32, name=f"esum_{t}") for t in range(8)]
        rsum = [keep.tile([P, 1], F32, name=f"rsum_{t}") for t in range(8)]

        nc.vector.memset(warm[:], 0.0)
        nc.vector.memset(eps[:], 1e-6)
        make_identity(nc, ident_f[:])
        nc.gpsimd.tensor_copy(out=ident_b[:], in_=ident_f[:])

        ctx.enter_context(tc.manual_schedule())

        mem_v = mem.rearrange("(c p i) w -> c p i w", p=P, i=4)
        out_v = out.rearrange("(c p i) w -> c p i w", p=P, i=4)
        key_v = key_bytes.rearrange("(g p j) w -> g p j w", p=P, j=J)
        er_v = erase.rearrange("(g p j) w -> g p j w", p=P, j=J)
        ad_v = add.rearrange("(g p j) w -> g p j w", p=P, j=J)
        ea_src = [er_v[0], ad_v[0], er_v[1], ad_v[1]]

        nc.vector.memset(gain_row[:], 0.0)
        nc.vector.memset(ones[:], 1.0)
        nc.scalar.dma_start(out=kscale[:], in_=key_scale.rearrange("o (p u e) -> p (o u) e", p=P, u=2))
        nc.scalar.dma_start(out=gain_row[0:1, :], in_=gm.rearrange("(o k) -> o k", o=1))
        nc.scalar.dma_start(out=s_raw[:], in_=s.rearrange("(g p j) -> p g j", p=P, j=J))
        nc.sync.dma_start(out=memt[0][:, 0:2, :], in_=mem_v[0][:, 0:2, :])
        nc.sync.dma_start(out=kbytes[0][:], in_=key_v[0])
        nc.sync.dma_start(out=memt[0][:, 2:4, :], in_=mem_v[0][:, 2:4, :])
        nc.sync.dma_start(out=memt[1][:], in_=mem_v[1])
        nc.sync.dma_start(out=ea_raw[0][:], in_=ea_src[0])
        nc.sync.dma_start(out=memt[2][:], in_=mem_v[2])
        nc.sync.dma_start(out=ea_raw[1][:], in_=ea_src[1])
        nc.sync.dma_start(out=memt[3][:], in_=mem_v[3])
        nc.sync.dma_start(out=kbytes[1][:], in_=key_v[1])
        nc.sync.dma_start(out=ea_raw[2][:], in_=ea_src[2])
        nc.sync.dma_start(out=ea_raw[3][:], in_=ea_src[3])
        nc.scalar.activation(out=warm_out[:], in_=warm[:], func=ACT.Sqrt)

        def sum_squares(c):
            for i in range(4):
                nc.scalar.activation(out=junk[:], in_=memt[c][:, i, :], func=ACT.Square, accum_out=sumsq[c][:, i : i + 1])

        def rnorms_s(c):
            nc.scalar.activation(out=length[c][:], in_=sumsq[c][:], func=ACT.Sqrt, bias=eps[:], scale=1.0)

        def rnorms_v(c):
            nc.vector.reciprocal(out=rnorm[c][:], in_=length[c][:])

        def transpose_in(rows):
            words = rows[:].rearrange("p i k -> p (i k)").bitcast(F32)
            banks = []
            for b in range(2):
                bank = psum.tile([P, 2, 2, P], F32, name="bank", tag="bank", bufs=8)
                for a in range(2):
                    for u in range(2):
                        i = 2 * b + a
                        nc.tensor.transpose(bank[:, a, u, :], words[:, 256 * i + u : 256 * (i + 1) : 2], ident_f[:])
                banks.append(bank)
            return banks

        def copy_grouped(banks, grouped, which):
            copy = nc.vector.tensor_copy if which in COPY_V else nc.scalar.copy
            gw = grouped[:].rearrange("p n j -> p (n j)").bitcast(F32)
            for b in range(2):
                copy(
                    out=gw[:, 512 * b : 512 * (b + 1)].rearrange("p (a r u) -> p a r u", a=2, u=2),
                    in_=banks[b][:].rearrange("p a u r -> p a r u"),
                )

        def quantize(grouped, codes, plane):
            nc.vector.quantize_mx(out=codes[:].bitcast(FP8X4), scales=plane[:], in_=grouped[:].rearrange("p n j -> p (n j)"))

        def key_widen(g):
            rows = ring.tile([P, J, W], BF16, name="key_rows", tag="rows", bufs=3)
            cast = nc.vector.tensor_copy if g == 0 else nc.scalar.copy
            cast(out=rows[:].rearrange("p j w -> p (j w)"), in_=kbytes[g][:].rearrange("p j w -> p (j w)").bitcast(FP8))
            return rows

        def key_scale_out(banks, g4):
            for b in range(2):
                for a in range(2):
                    n0 = 128 * (2 * b + a)
                    nc.vector.tensor_tensor(
                        out=g4[:, n0 : n0 + 128, :].rearrange("p r (u e) -> p r u e", u=2),
                        in0=banks[b][:, a, :, :].bitcast(BF16).rearrange("p u (r e) -> p r u e", e=2),
                        in1=kscale[:].unsqueeze(1).to_broadcast([P, P, 2, 2]),
                        op=ALU.mult,
                    )

        def mem_norm(c):
            rows = ring.tile([P, J, W], BF16, name="mem_rows", tag="rows", bufs=3)
            for i in range(4):
                nc.vector.scalar_tensor_tensor(
                    out=rows[:, i, :], in0=memt[c][:, i, :], scalar=rnorm[c][:, i : i + 1], in1=gain[:], op0=ALU.mult, op1=ALU.mult
                )
            return rows

        def new_grouped():
            g4 = ring.tile([P, 512, 4], BF16, name="grouped", tag="grouped", bufs=6, align_bytes=64)
            return g4

        cl = {}

        def logits(t, chunks=range(C)):
            g, j = divmod(t, J)
            for c in chunks:
                bank = psum.tile([P, 512], F32, name="bank", tag="bank", bufs=8)
                nc.tensor.matmul_mx(
                    out=bank[:],
                    lhsT=kcodes[g][:, 128 * j : 128 * (j + 1)].bitcast(FP8X4),
                    lhsT_scale=kplane[g][:, 128 * j : 128 * (j + 1)],
                    rhs=mcodes[c][:].bitcast(FP8X4),
                    rhs_scale=mplane[c][:],
                    start=True,
                    stop=True,
                )
                cl[t, c] = bank

        def bank_max(t, c):
            nc.vector.tensor_reduce(out=negmax4[t][:, c : c + 1], in_=cl[t, c][:], axis=X, op=ALU.max, negate=True)

        def row_max(t):
            nc.vector.tensor_reduce(out=negmax[t][:], in_=negmax4[t][:], axis=X, op=ALU.min)

        exps = {}

        def exponentials(t):
            e = ring.tile([P, C, 512], F32, name="e", tag="e", bufs=3)
            exps[t] = e
            for c in range(C):
                nc.scalar.activation(
                    out=e[:, c, :], in_=cl[t, c][:], func=ACT.Exp, bias=negmax[t][:], scale=1.0, accum_out=esum4[t][:, c : c + 1]
                )

        def row_sum(t):
            nc.vector.tensor_reduce(out=esum[t][:], in_=esum4[t][:], axis=X, op=ALU.add)

        def row_recip(t):
            nc.vector.reciprocal(out=rsum[t][:], in_=esum[t][:])

        def weights(t, engine, chunks):
            g, j = divmod(t, J)
            for c in chunks:
                engine.tensor_scalar(
                    out=w_bf[g][c][:, j, :], in0=exps[t][:, c, :], scalar1=rsum[t][:], scalar2=s64[:, t : t + 1], op0=ALU.mult, op1=ALU.mult
                )

        def pe_interleave(rows):
            banks = []
            for h in range(2):
                bank = psum.tile([P, 2, P, J], BF16, name="ilbank", tag="bank", bufs=8)
                for q in range(2):
                    col = 256 * h + 128 * q
                    nc.tensor.matmul(
                        out=bank[:, q, :, :],
                        lhsT=ident_b[:],
                        rhs=rows[:, :, col : col + 128].rearrange("p j n -> p n j"),
                        start=True,
                        stop=True,
                    )
                banks.append(bank)
            return banks

        def copy_interleaved(banks, g4, h, copy):
            copy(
                out=g4[:, 256 * h : 256 * (h + 1), :].rearrange("p n j -> p (n j)"), in_=banks[h][:].rearrange("p q n j -> p (q n j)")
            )

        def w_interleave(copy, g, c, g4, h):
            copy(out=g4[:, 256 * h : 256 * (h + 1), :], in_=w_bf[g][c][:, :, 256 * h : 256 * (h + 1)].rearrange("p j n -> p n j"))

        def quantize_half(g4, codes, plane, h):
            nc.vector.quantize_mx(
                out=codes[:, 256 * h : 256 * (h + 1)].bitcast(FP8X4),
                scales=plane[:, 256 * h : 256 * (h + 1)],
                in_=g4[:, 256 * h : 256 * (h + 1), :].rearrange("p n j -> p (n j)"),
            )

        SS, VV = nc.scalar.copy, nc.vector.tensor_copy
        kb, kgrp, mb, mgrp, eab, eag, wb, wg = {}, {}, {}, {}, {}, {}, {}, {}

        def copy_out(kind, x):
            if kind == "k":
                kgrp[x] = new_grouped()
                key_scale_out(kb[x], kgrp[x])
            else:
                mgrp[x] = new_grouped()
                copy_grouped(mb[x], mgrp[x], f"{kind}{x}")

        def ea_pe(i):
            eab[i] = pe_interleave(ea_raw[i])

        def ea_copy(i, engines=None):
            engines = engines or (SS, SS)
            eag[i] = new_grouped()
            for h in range(2):
                copy_interleaved(eab[i], eag[i], h, engines[h])

        def ea_quant(i):
            quantize(eag[i], eacodes[i], eaplane[i])

        def w_pe(c):
            wb[c] = pe_interleave(w_bf[0][c])

        def w_copy(c, engines=None):
            engines = engines or (SS, SS)
            wg[c] = new_grouped()
            for h in range(2):
                copy_interleaved(wb[c], wg[c], h, engines[h])

        def w_quant(c):
            quantize(wg[c], wcodes[0][c], wplane[0][c])

        gbank = psum.tile([P, W], F32, name="gbank", tag="bank", bufs=8)
        nc.tensor.matmul(out=gbank[:], lhsT=ones[:], rhs=gain_row[:], start=True, stop=True)
        krows0 = key_widen(0)
        nc.vector.tensor_copy(out=gain[:], in_=gbank[:])
        sum_squares(0)
        rnorms_s(0)
        sum_squares(1)
        rnorms_s(1)
        kb[0] = transpose_in(krows0)
        copy_out("k", 0)
        rnorms_v(0)
        mb[0] = transpose_in(mem_norm(0))
        quantize(kgrp[0], kcodes[0], kplane[0])
        nc.gpsimd.tensor_scalar(
            out=s64[:], in0=s_raw[:].rearrange("p g j -> p (g j)"), scalar1=64.0, scalar2=0.0, op0=ALU.mult, op1=ALU.add
        )
        sum_squares(2)
        rnorms_s(2)
        copy_out("m", 0)
        rnorms_v(1)
        mb[1] = transpose_in(mem_norm(1))
        sum_squares(3)
        rnorms_s(3)
        rnorms_v(2)
        mb[2] = transpose_in(mem_norm(2))
        quantize(mgrp[0], mcodes[0], mplane[0])
        copy_out("m", 1)
        nc.scalar.activation(out=warm_out[:], in_=warm[:], func=ACT.Exp)
        ea_pe(0)
        krows1 = key_widen(1)
        rnorms_v(3)
        logits(0, [0])
        mb[3] = transpose_in(mem_norm(3))
        copy_out("m", 2)
        quantize(mgrp[1], mcodes[1], mplane[1])
        ea_copy(0)
        copy_out("m", 3)
        quantize(mgrp[2], mcodes[2], mplane[2])
        logits(0, [1, 2])
        kb[1] = transpose_in(krows1)
        bank_max(0, 0)
        bank_max(0, 1)
        quantize(mgrp[3], mcodes[3], mplane[3])
        bank_max(0, 2)
        logits(0, [3])
        ea_pe(1)
        ea_copy(1)
        for t in range(8):
            for c in range(C):
                if (t, c) not in ((0, 0), (0, 1), (0, 2)):
                    bank_max(t, c)
            if t > 0:
                row_sum(t - 1)
            row_max(t)
            if t > 0:
                row_recip(t - 1)
                weights(t - 1, nc.gpsimd, range(C))
            if t + 1 < 8:
                logits(t + 1)
            exponentials(t)
            if t == 0:
                copy_out("k", 1)
            if t == 1:
                quantize(kgrp[1], kcodes[1], kplane[1])
            if 1 <= t <= 2:
                ea_pe(t + 1)
                ea_copy(t + 1)
            if 2 <= t <= 5:
                ea_quant(t - 2)
            if t >= 5:
                w_pe(t - 5)
                w_copy(t - 5)
            if t == 7:
                w_quant(0)
        w_pe(3)
        w_copy(3)
        row_sum(7)
        row_recip(7)
        grp = {}
        weights(7, nc.vector, range(0, 2))
        grp[1, 0] = new_grouped()
        w_interleave(VV, 1, 0, grp[1, 0], 0)
        grp[1, 1] = new_grouped()
        w_interleave(SS, 1, 1, grp[1, 1], 0)
        w_interleave(SS, 1, 1, grp[1, 1], 1)
        quantize_half(grp[1, 0], wcodes[1][0], wplane[1][0], 0)
        weights(7, nc.vector, range(2, 4))
        w_interleave(VV, 1, 0, grp[1, 0], 1)
        quantize_half(grp[1, 0], wcodes[1][0], wplane[1][0], 1)
        w_quant(1)

        acc = {}

        def open_tile(m):
            for k in range(2):
                acc[m, k] = psum.tile([P, 512], F32, name="acc", tag="bank", bufs=8)

        def write_pass(m, g):
            c, i = divmod(m, 4)
            for k in range(2):
                nc.tensor.matmul_mx(
                    out=acc[m, k][:],
                    lhsT=wcodes[g][c][:, 128 * i : 128 * (i + 1)].bitcast(FP8X4),
                    lhsT_scale=wplane[g][c][:, 128 * i : 128 * (i + 1)],
                    rhs=eacodes[2 * g + k][:].bitcast(FP8X4),
                    rhs_scale=eaplane[2 * g + k][:],
                    start=(g == 0),
                    stop=(g == 1),
                )

        erased = {}
        results = {}

        def finish_a(m):
            c, i = divmod(m, 4)
            if i % 2 == 0:
                results[m // 2] = ring.tile([P, 2, 512], F32, name="result", tag="result", bufs=3)
            erased[m] = ring.tile([P, 512], F32, name="erased", tag="erased", bufs=4)
            nc.vector.scalar_tensor_tensor(
                out=erased[m][:], in0=acc[m, 0][:], scalar=1.0, in1=memt[c][:, i, :], op0=ALU.subtract, op1=ALU.mult
            )
            if m in OP2_GPSIMD:
                added = ring.tile([P, 512], F32, name="added", tag="added", bufs=3)
                nc.scalar.copy(out=added[:], in_=acc[m, 1][:])
                acc[m, 1] = added

        def finish_b(m):
            c, i = divmod(m, 4)
            engine = nc.gpsimd if m in OP2_GPSIMD else nc.vector
            engine.tensor_tensor(out=results[m // 2][:, i % 2, :], in0=acc[m, 1][:], in1=erased[m][:], op=ALU.subtract)
            if m >= 14:
                nc.sync.dma_start(out=out_v[c][:, i, :], in_=results[m // 2][:, i % 2, :])
            elif i % 2 == 1:
                nc.sync.dma_start(out=out_v[c][:, i - 1 : i + 1, :], in_=results[m // 2][:])

        for m in range(4):
            open_tile(m)
            write_pass(m, 0)
        for m in range(NTILES):
            c, i = divmod(m, 4)
            if m >= 4:
                open_tile(m)
                write_pass(m, 0)
            write_pass(m, 1)
            if i == 1 and c + 1 < C:
                quantize(grp[1, c + 1], wcodes[1][c + 1], wplane[1][c + 1])
            finish_a(m)
            if m > 0:
                finish_b(m - 1)
            if m in (2, 5):
                w_quant(2 if m == 2 else 3)
            if m in (0, 1, 2, 3):
                nxt = 2 if m < 2 else 3
                if m in (0, 2):
                    grp[1, nxt] = new_grouped()
                w_interleave(SS, 1, nxt, grp[1, nxt], m % 2)
        finish_b(15)
